import numpy as np
import ml_dtypes


def mxq(x, axis, fmt="e4m3"):
    dtype, down = {"e4m3": (ml_dtypes.float8_e4m3fn, 7), "e5m2": (ml_dtypes.float8_e5m2, 14)}[fmt]
    v = np.moveaxis(np.asarray(x, np.float32).astype(ml_dtypes.bfloat16).astype(np.float64), axis, -1)
    blocks = v.reshape(v.shape[:-1] + (-1, 32))
    amax = np.abs(blocks).max(-1, keepdims=True)
    byte = np.maximum(np.where(amax > 0, np.frexp(amax)[1] - 1 + 127, 0) - down, 1)
    scale = np.exp2(byte - 127.0)
    codes = (blocks / scale).astype(np.float32).astype(dtype).astype(np.float64)
    return np.moveaxis((codes * scale).reshape(v.shape), -1, axis)


WIDE = False


def mx_kscale(k):
    if not WIDE:
        return np.ones(k)
    levels = np.array([24, -24, 12, -12, 0])
    if k % 512:
        return np.exp2(np.random.permutation(np.resize(levels, k // 32))).repeat(32)
    a = np.empty((k // 512, 16))
    for p in range(k // 512):
        a[p, :8] = np.random.permutation(np.resize(levels, 8))
        for g in range(8):
            far = levels[np.abs(levels - a[p, g]) >= 10]
            a[p, g + 8] = far[np.random.randint(len(far))]
    return np.exp2(a.ravel()).repeat(32)


def f64(x):
    return np.asarray(x).astype(np.float64)


def striped(idx):
    return np.tile(idx.reshape(-1, 16).T, (8, 1)).astype(np.uint16)


def unstriped(offs):
    return offs[:16].T.reshape(-1).astype(np.int64)


E2M1 = np.array([0.0, 0.5, 1.0, 1.5, 2.0, 3.0, 4.0, 6.0, -0.0, -0.5, -1.0, -1.5, -2.0, -3.0, -4.0, -6.0])


def pack_weight(w, fmt):
    k, n = w.shape
    w = f64(np.asarray(w, np.float32).astype(ml_dtypes.bfloat16)).reshape(k // 32, 32, n)
    amax = np.abs(w).max(1)
    if fmt == "e4m3":
        byte = np.frexp(amax)[1] - 1 + 127 - 7
    else:
        mant, ex = np.frexp(amax / 6.0)
        byte = np.where(mant > 0.5, ex, ex - 1) + 127
    byte = np.clip(np.where(amax > 0, byte, 1), 1, 254)
    scaled = (w * np.exp2(127.0 - byte)[:, None, :]).reshape(k, n).astype(np.float32)
    by_word = np.ascontiguousarray(scaled.reshape(k // 512, 128, 4, n).transpose(0, 1, 3, 2))
    if fmt == "e4m3":
        words = by_word.astype(ml_dtypes.float8_e4m3fn).view(np.uint8)
    else:
        c = by_word.astype(ml_dtypes.float4_e2m1fn).view(np.uint8) & 0xF
        words = (c[..., 0::2] | (c[..., 1::2] << 4)).reshape(k // 512, 128, 2 * n)
    return np.ascontiguousarray(words), np.ascontiguousarray(byte.astype(np.uint8).reshape(k // 512, 16, n))


def unpack_weight(words, scales, fmt):
    g, _, n = scales.shape
    words = np.ascontiguousarray(words).reshape(g, 128, n, -1)
    if fmt == "e4m3":
        vals = words.view(ml_dtypes.float8_e4m3fn).astype(np.float64)
    else:
        nib = np.empty((g, 128, n, 4), np.uint8)
        nib[..., 0::2] = words & 0xF
        nib[..., 1::2] = words >> 4
        vals = E2M1[nib]
    vals = vals * np.repeat(np.exp2(scales.astype(np.float64) - 127.0), 8, axis=1)[..., None]
    return vals.transpose(0, 1, 3, 2).reshape(g * 512, n)


def pack_table4(v):
    words, scales = pack_weight(v, "e2m1")
    g, t = words.shape[0] // 2, v.shape[1]
    return np.ascontiguousarray(words.reshape(g, 2, 128, t, 2).transpose(0, 2, 3, 1, 4).reshape(g, 128, t, 4)), scales


def unpack_table4(words, scales):
    g, _, t, _ = words.shape
    return unpack_weight(words.reshape(g, 128, t, 2, 2).transpose(0, 3, 1, 2, 4).reshape(2 * g, 128, 2 * t), scales, "e2m1")


K, N, T, J = 1024, 512, 2048, 1024


def setup_inputs():
    n = np.random.standard_normal
    s = mx_kscale(K)[:, None]
    p_tab = pack_table4(n((K, T)) * s)
    p_tab2 = pack_table4(n((K, T)) * s)
    p_wr4 = pack_weight(n((K, N)) / np.sqrt(2 * K) / s, "e2m1")
    p_wi = pack_weight(n((K, N)) / np.sqrt(2 * K) / s, "e4m3")
    return {
        "tab_words": p_tab[0],
        "tab_scales": p_tab[1],
        "tab2_words": p_tab2[0],
        "tab2_scales": p_tab2[1],
        "wr4_words": p_wr4[0],
        "wr4_scales": p_wr4[1],
        "wrd": (0.4 * (n((K, N)) / np.sqrt(2 * K) / s)).astype(np.float32),
        "wi_words": p_wi[0],
        "wi_scales": p_wi[1],
        "offs": striped(np.random.permutation(T)[:J]),
    }


def reference(tab_words, tab_scales, tab2_words, tab2_scales, wr4_words, wr4_scales, wrd, wi_words, wi_scales, offs):
    idx = unstriped(offs)
    tab_ = unpack_table4(tab_words, tab_scales)[:, idx]
    tab2_ = unpack_table4(tab2_words, tab2_scales)[:, idx]
    wr4_ = unpack_weight(wr4_words, wr4_scales, "e2m1")
    wrd_ = mxq(f64(wrd), 0, "e4m3")
    wi_ = unpack_weight(wi_words, wi_scales, "e4m3")
    rr = wr4_.T @ tab_ + wrd_.T @ tab_
    ii = wi_.T @ tab2_
    zr = rr - ii
    ri = wr4_.T @ tab2_ + wrd_.T @ tab2_ + wi_.T @ tab_
    zi = ri
    return np.maximum(zr, 0.0), np.maximum(zi, 0.0)

@@ -1,0 +1,180 @@
+from contextlib import ExitStack
+
+import concourse.mybir as mybir
+
+K, N, T, J = 1024, 512, 2048, 1024
+FLOPS = 6 * 2 * K * N * J
+
+F32 = mybir.dt.float32
+BF16 = mybir.dt.bfloat16
+I32 = mybir.dt.int32
+U32 = mybir.dt.uint32
+U16 = mybir.dt.uint16
+U8 = mybir.dt.uint8
+FP8X4 = mybir.dt.float8_e4m3fn_x4
+FP4X4 = mybir.dt.float4_e2m1fn_x4
+ACT = mybir.ActivationFunctionType
+ALU = mybir.AluOpType
+
+P = 128
+PASSES = 2
+M_TILE = 128
+N_TILES = N // M_TILE
+HALF = 512
+HALVES = J // HALF
+
+
+def tile_list_cpxtab_dl_crelu_kernel(
+    tc, tab_words, tab_scales, tab2_words, tab2_scales, wr4_words, wr4_scales, wrd, wi_words, wi_scales, offs,
+    out_0, out_1,
+):
+    nc = tc.nc
+    with ExitStack() as ctx:
+        keep = ctx.enter_context(tc.tile_pool(name="keep", bufs=1))
+        outs = ctx.enter_context(tc.tile_pool(name="outs", bufs=4))
+        psum = ctx.enter_context(tc.psum_pool(name="psum", bufs=8))
+
+        offsets = keep.tile([P, J // 16], U16, name="offsets")
+
+        def zeroed_plane(name, width):
+            plane = keep.tile([P, PASSES, width], U8, name=name, align_bytes=64)
+            nc.vector.memset(plane[:].bitcast(I32), 0)
+            return plane
+
+        def load_scale_rows(plane, scales, queue):
+            for q in range(4):
+                queue.dma_start(
+                    out=plane[32 * q : 32 * q + 4, :, :].bitcast(I32),
+                    in_=scales[:, 4 * q : 4 * q + 4, :].rearrange("a r c -> r a c").bitcast(I32),
+                )
+
+        def load_table_words(name, words):
+            window = keep.tile([P, T], I32, name=name, align_bytes=64)
+            nc.sync.dma_start(out=window[:], in_=words[0].rearrange("p t b -> p (t b)").bitcast(I32))
+            return window
+
+        wr4_planes = zeroed_plane("wr4_planes", N)
+        v2_planes = zeroed_plane("v2_planes", T)
+        wi_planes = zeroed_plane("wi_planes", N)
+        v_planes = zeroed_plane("v_planes", T)
+
+        nc.sync.dma_start(offsets[:], offs)
+        v2_window = load_table_words("v2_window", tab2_words)
+        load_scale_rows(wr4_planes, wr4_scales, nc.sync)
+        load_scale_rows(v2_planes, tab2_scales, nc.sync)
+        wr4_codes = keep.tile([P, PASSES, 2 * N], U8, name="wr4_codes", align_bytes=64)
+        nc.sync.dma_start(out=wr4_codes[:].bitcast(I32), in_=wr4_words.rearrange("a p c -> p a c").bitcast(I32))
+        wi_codes = keep.tile([P, PASSES, 4 * N], U8, name="wi_codes", align_bytes=64)
+        nc.sync.dma_start(out=wi_codes[:].bitcast(I32), in_=wi_words.rearrange("a p n i -> p a (n i)").bitcast(I32))
+        load_scale_rows(wi_planes, wi_scales, nc.sync)
+        v_window = load_table_words("v_window", tab_words)
+        load_scale_rows(v_planes, tab_scales, nc.sync)
+        wrd_raw = []
+        for a in range(PASSES):
+            raw = keep.tile([P, 4, N], F32, name=f"wrd_raw{a}")
+            nc.sync.dma_start(out=raw[:], in_=wrd[512 * a : 512 * (a + 1), :].rearrange("(p i) n -> p i n", i=4))
+            wrd_raw.append(raw)
+
+        def gather(name, window, planes, h):
+            entries = offsets[:, h * HALF // 16 : (h + 1) * HALF // 16]
+            words = keep.tile([P, HALF], U32, name=f"{name}_words{h}", align_bytes=64)
+            nc.vector.tensor_copy(words[:], window[:].bitcast(U32).indirect(entries))
+            parted = keep.tile([P, PASSES, 2 * HALF], U8, name=f"{name}_parted{h}", align_bytes=64)
+            nc.vector.tensor_copy(
+                parted[:].bitcast(U16), words[:].bitcast(U16).rearrange("p (j a) -> p a j", a=PASSES)
+            )
+            scales = []
+            for a in range(PASSES):
+                picked = keep.tile([P, HALF], U8, name=f"{name}_scales{h}{a}", align_bytes=64)
+                nc.vector.tensor_copy(picked[:], planes[:, a, :].indirect(entries))
+                scales.append(picked)
+            return [(parted[:, a, :].bitcast(FP4X4), scales[a][:]) for a in range(PASSES)]
+
+        wrd_codes = keep.tile([P, PASSES, N], U32, name="wrd_codes", align_bytes=64)
+        wrd_planes = keep.tile([P, PASSES, N], U8, name="wrd_planes", align_bytes=64)
+
+        def quantise_wrd():
+            grouped = []
+            for a in range(PASSES):
+                g = keep.tile([P, N, 4], BF16, name=f"wrd_grouped{a}", align_bytes=64)
+                nc.scalar.copy(g[:], wrd_raw[a][:].rearrange("p i n -> p n i"))
+                grouped.append(g)
+            for a in range(PASSES):
+                nc.vector.quantize_mx(
+                    out=wrd_codes[:, a, :].bitcast(FP8X4),
+                    scales=wrd_planes[:, a, :],
+                    in_=grouped[a][:].rearrange("p n i -> p (n i)"),
+                )
+
+        def wi(a, n):
+            return wi_codes[:, a, 4 * M_TILE * n : 4 * M_TILE * (n + 1)].bitcast(FP8X4), wi_planes[:, a, M_TILE * n : M_TILE * (n + 1)]
+
+        def wr4(a, n):
+            return wr4_codes[:, a, 2 * M_TILE * n : 2 * M_TILE * (n + 1)].bitcast(FP4X4), wr4_planes[:, a, M_TILE * n : M_TILE * (n + 1)]
+
+        def wrd8(a, n):
+            return wrd_codes[:, a, M_TILE * n : M_TILE * (n + 1)].bitcast(FP8X4), wrd_planes[:, a, M_TILE * n : M_TILE * (n + 1)]
+
+        def product(acc, weight, n, columns, start=False, stop=False):
+            for a in range(PASSES):
+                codes, scales = weight(a, n)
+                nc.tensor.matmul_mx(
+                    out=acc[:], lhsT=codes, lhsT_scale=scales, rhs=columns[a][0], rhs_scale=columns[a][1],
+                    start=start and a == 0, stop=stop and a == PASSES - 1,
+                )
+
+        ii = {}
+
+        def make_ii(h, v2):
+            for n in range(N_TILES):
+                acc = psum.tile([P, HALF], F32, name="acc")
+                product(acc, wi, n, v2, start=True, stop=True)
+                ii[h, n] = keep.tile([P, HALF], F32, name=f"ii{h}{n}")
+                nc.scalar.copy(ii[h, n][:], acc[:])
+
+        def finish_real(acc, h, n):
+            zr = outs.tile([P, HALF], F32, name="zr")
+            nc.vector.tensor_tensor(zr[:], acc[:], ii[h, n][:], ALU.subtract)
+            res = outs.tile([P, HALF], F32, name="res0")
+            nc.scalar.activation(res[:], zr[:], ACT.Relu)
+            nc.sync.dma_start(out=out_0[M_TILE * n : M_TILE * (n + 1), HALF * h : HALF * (h + 1)], in_=res[:])
+
+        def finish_imag(acc, h, n):
+            res = outs.tile([P, HALF], F32, name="res1")
+            nc.scalar.activation(res[:], acc[:], ACT.Relu)
+            nc.sync.dma_start(out=out_1[M_TILE * n : M_TILE * (n + 1), HALF * h : HALF * (h + 1)], in_=res[:])
+
+        v2_0 = gather("v2", v2_window, v2_planes, 0)
+        ri = []
+        for n in range(N_TILES):
+            acc = psum.tile([P, HALF], F32, name="acc")
+            product(acc, wr4, n, v2_0, start=True)
+            ri.append(acc)
+        make_ii(0, v2_0)
+        v2_1 = gather("v2", v2_window, v2_planes, 1)
+        make_ii(1, v2_1)
+        v_0 = gather("v", v_window, v_planes, 0)
+        for n in range(N_TILES):
+            product(ri[n], wi, n, v_0)
+        rr = []
+        for n in range(N_TILES):
+            acc = psum.tile([P, HALF], F32, name="acc")
+            product(acc, wr4, n, v_0, start=True)
+            rr.append(acc)
+        quantise_wrd()
+        v_1 = gather("v", v_window, v_planes, 1)
+        for n in range(N_TILES):
+            product(rr[n], wrd8, n, v_0, stop=True)
+            finish_real(rr[n], 0, n)
+            product(ri[n], wrd8, n, v2_0, stop=True)
+            finish_imag(ri[n], 0, n)
+        for n in range(N_TILES):
+            acc = psum.tile([P, HALF], F32, name="acc")
+            product(acc, wr4, n, v_1, start=True)
+            product(acc, wrd8, n, v_1, stop=True)
+            finish_real(acc, 1, n)
+            acc = psum.tile([P, HALF], F32, name="acc")
+            product(acc, wr4, n, v2_1, start=True)
+            product(acc, wrd8, n, v2_1)
+            product(acc, wi, n, v_1, stop=True)
+            finish_imag(acc, 1, n)

@@ -36,13 +36,13 @@ def tile_list_cpxtab_dl_crelu_kernel(
 
         offsets = keep.tile([P, J // 16], U16, name="offsets")
 
-        def zeroed_plane(name, width):
+        def zeroed_plane(name, width, engine):
             plane = keep.tile([P, PASSES, width], U8, name=name, align_bytes=64)
-            nc.vector.memset(plane[:].bitcast(I32), 0)
+            engine.memset(plane[:].bitcast(I32), 0)
             return plane
 
-        def load_scale_rows(plane, scales, queue):
-            for q in range(4):
+        def load_scale_rows(plane, scales, queue, quadrants=range(4)):
+            for q in quadrants:
                 queue.dma_start(
                     out=plane[32 * q : 32 * q + 4, :, :].bitcast(I32),
                     in_=scales[:, 4 * q : 4 * q + 4, :].rearrange("a r c -> r a c").bitcast(I32),
@@ -53,57 +53,64 @@ def tile_list_cpxtab_dl_crelu_kernel(
             nc.sync.dma_start(out=window[:], in_=words[0].rearrange("p t b -> p (t b)").bitcast(I32))
             return window
 
-        wr4_planes = zeroed_plane("wr4_planes", N)
-        v2_planes = zeroed_plane("v2_planes", T)
-        wi_planes = zeroed_plane("wi_planes", N)
-        v_planes = zeroed_plane("v_planes", T)
+        wr4_planes = zeroed_plane("wr4_planes", N, nc.gpsimd)
+        v2_planes = zeroed_plane("v2_planes", T, nc.vector)
+        v_planes = zeroed_plane("v_planes", T, nc.vector)
+        wi_planes = zeroed_plane("wi_planes", N, nc.vector)
 
         nc.sync.dma_start(offsets[:], offs)
         v2_window = load_table_words("v2_window", tab2_words)
-        load_scale_rows(wr4_planes, wr4_scales, nc.sync)
-        load_scale_rows(v2_planes, tab2_scales, nc.sync)
         wr4_codes = keep.tile([P, PASSES, 2 * N], U8, name="wr4_codes", align_bytes=64)
         nc.sync.dma_start(out=wr4_codes[:].bitcast(I32), in_=wr4_words.rearrange("a p c -> p a c").bitcast(I32))
-        wi_codes = keep.tile([P, PASSES, 4 * N], U8, name="wi_codes", align_bytes=64)
-        nc.sync.dma_start(out=wi_codes[:].bitcast(I32), in_=wi_words.rearrange("a p n i -> p a (n i)").bitcast(I32))
-        load_scale_rows(wi_planes, wi_scales, nc.sync)
+        load_scale_rows(wr4_planes, wr4_scales, nc.sync, range(0, 2))
+        load_scale_rows(wr4_planes, wr4_scales, nc.gpsimd, range(2, 4))
+        load_scale_rows(v2_planes, tab2_scales, nc.sync)
+        load_scale_rows(wi_planes, wi_scales, nc.gpsimd, range(2, 4))
         v_window = load_table_words("v_window", tab_words)
         load_scale_rows(v_planes, tab_scales, nc.sync)
-        wrd_raw = []
-        for a in range(PASSES):
-            raw = keep.tile([P, 4, N], F32, name=f"wrd_raw{a}")
-            nc.sync.dma_start(out=raw[:], in_=wrd[512 * a : 512 * (a + 1), :].rearrange("(p i) n -> p i n", i=4))
-            wrd_raw.append(raw)
+        wi_codes = keep.tile([P, PASSES, 4 * N], U8, name="wi_codes", align_bytes=64)
+        nc.sync.dma_start(out=wi_codes[:].bitcast(I32), in_=wi_words.rearrange("a p n i -> p a (n i)").bitcast(I32))
+        load_scale_rows(wi_planes, wi_scales, nc.sync, range(0, 2))
 
-        def gather(name, window, planes, h):
-            entries = offsets[:, h * HALF // 16 : (h + 1) * HALF // 16]
-            words = keep.tile([P, HALF], U32, name=f"{name}_words{h}", align_bytes=64)
-            nc.vector.tensor_copy(words[:], window[:].bitcast(U32).indirect(entries))
-            parted = keep.tile([P, PASSES, 2 * HALF], U8, name=f"{name}_parted{h}", align_bytes=64)
+        def entries(h, cols):
+            return offsets[:, (h * HALF + cols.start) // 16 : (h * HALF + cols.stop) // 16]
+
+        def gather_words(parted, window, h, cols, tag):
+            words = keep.tile([P, cols.stop - cols.start], U32, name="words", tag=tag, align_bytes=64)
+            nc.vector.tensor_copy(words[:], window[:].bitcast(U32).indirect(entries(h, cols)))
             nc.vector.tensor_copy(
-                parted[:].bitcast(U16), words[:].bitcast(U16).rearrange("p (j a) -> p a j", a=PASSES)
+                parted[:].bitcast(U16)[:, :, cols], words[:].bitcast(U16).rearrange("p (j a) -> p a j", a=PASSES)
             )
-            scales = []
-            for a in range(PASSES):
-                picked = keep.tile([P, HALF], U8, name=f"{name}_scales{h}{a}", align_bytes=64)
-                nc.vector.tensor_copy(picked[:], planes[:, a, :].indirect(entries))
-                scales.append(picked)
-            return [(parted[:, a, :].bitcast(FP4X4), scales[a][:]) for a in range(PASSES)]
+
+        def gather_scales(picked, planes, a, h, cols):
+            nc.vector.tensor_copy(picked[:, cols], planes[:, a, :].indirect(entries(h, cols)))
+
+        def parted_tile(name):
+            return keep.tile([P, PASSES, 2 * HALF], U8, name=name, align_bytes=64)
+
+        def picked_tile(tag):
+            return keep.tile([P, HALF], U8, name="picked", tag=tag, align_bytes=64)
 
         wrd_codes = keep.tile([P, PASSES, N], U32, name="wrd_codes", align_bytes=64)
         wrd_planes = keep.tile([P, PASSES, N], U8, name="wrd_planes", align_bytes=64)
 
-        def quantise_wrd():
-            grouped = []
+        wrd_raw = []
+
+        def load_wrd():
             for a in range(PASSES):
-                g = keep.tile([P, N, 4], BF16, name=f"wrd_grouped{a}", align_bytes=64)
-                nc.scalar.copy(g[:], wrd_raw[a][:].rearrange("p i n -> p n i"))
-                grouped.append(g)
-            for a in range(PASSES):
+                raw = keep.tile([P, 4, N], F32, name=f"wrd_raw{a}", tag=f"raw{a}", align_bytes=64)
+                nc.sync.dma_start(out=raw[:], in_=wrd[512 * a : 512 * (a + 1), :].rearrange("(p i) n -> p i n", i=4))
+                wrd_raw.append(raw)
+
+        def quantise_wrd(a):
+            for u in range(2):
+                cols = slice(u * N // 2, (u + 1) * N // 2)
+                g = keep.tile([P, N // 2, 4], BF16, name="grouped", tag=f"grouped{a}{u}", align_bytes=64)
+                nc.scalar.copy(g[:], wrd_raw[a][:, :, cols].rearrange("p i n -> p n i"))
                 nc.vector.quantize_mx(
-                    out=wrd_codes[:, a, :].bitcast(FP8X4),
-                    scales=wrd_planes[:, a, :],
-                    in_=grouped[a][:].rearrange("p n i -> p (n i)"),
+                    out=wrd_codes[:, a, cols].bitcast(FP8X4),
+                    scales=wrd_planes[:, a, cols],
+                    in_=g[:].rearrange("p n i -> p (n i)"),
                 )
 
         def wi(a, n):
@@ -115,13 +122,18 @@ def tile_list_cpxtab_dl_crelu_kernel(
         def wrd8(a, n):
             return wrd_codes[:, a, M_TILE * n : M_TILE * (n + 1)].bitcast(FP8X4), wrd_planes[:, a, M_TILE * n : M_TILE * (n + 1)]
 
+        def one_pass(acc, weight, a, n, columns, start=False, stop=False, cols=slice(0, HALF)):
+            codes, scales = weight(a, n)
+            parted, picked = columns
+            nc.tensor.matmul_mx(
+                out=acc[:, cols], lhsT=codes, lhsT_scale=scales,
+                rhs=parted[:, a, 2 * cols.start : 2 * cols.stop].bitcast(FP4X4), rhs_scale=picked[a][:, cols],
+                start=start, stop=stop,
+            )
+
         def product(acc, weight, n, columns, start=False, stop=False):
             for a in range(PASSES):
-                codes, scales = weight(a, n)
-                nc.tensor.matmul_mx(
-                    out=acc[:], lhsT=codes, lhsT_scale=scales, rhs=columns[a][0], rhs_scale=columns[a][1],
-                    start=start and a == 0, stop=stop and a == PASSES - 1,
-                )
+                one_pass(acc, weight, a, n, columns, start and a == 0, stop and a == PASSES - 1)
 
         ii = {}
 
@@ -136,7 +148,10 @@ def tile_list_cpxtab_dl_crelu_kernel(
             zr = outs.tile([P, HALF], F32, name="zr")
             nc.vector.tensor_tensor(zr[:], acc[:], ii[h, n][:], ALU.subtract)
             res = outs.tile([P, HALF], F32, name="res0")
-            nc.scalar.activation(res[:], zr[:], ACT.Relu)
+            if h == 0:
+                nc.scalar.activation(res[:], zr[:], ACT.Relu)
+            else:
+                nc.vector.tensor_scalar_max(res[:], zr[:], 0.0)
             nc.sync.dma_start(out=out_0[M_TILE * n : M_TILE * (n + 1), HALF * h : HALF * (h + 1)], in_=res[:])
 
         def finish_imag(acc, h, n):
@@ -144,37 +159,72 @@ def tile_list_cpxtab_dl_crelu_kernel(
             nc.scalar.activation(res[:], acc[:], ACT.Relu)
             nc.sync.dma_start(out=out_1[M_TILE * n : M_TILE * (n + 1), HALF * h : HALF * (h + 1)], in_=res[:])
 
-        v2_0 = gather("v2", v2_window, v2_planes, 0)
-        ri = []
+        whole = slice(0, HALF)
+        pieces = [slice(0, HALF // 2), slice(HALF // 2, HALF)]
+
+        v2_0 = (parted_tile("v2_parted0"), [picked_tile("v2_00"), picked_tile("v2_01")])
+        for i, cols in enumerate(pieces):
+            gather_words(v2_0[0], v2_window, 0, cols, f"raw{i}")
+            gather_scales(v2_0[1][0], v2_planes, 0, 0, cols)
+        gather_scales(v2_0[1][1], v2_planes, 1, 0, whole)
+        load_wrd()
+        ri = [psum.tile([P, HALF], F32, name="acc") for n in range(N_TILES)]
+        for i, cols in enumerate(pieces):
+            for n in range(N_TILES):
+                one_pass(ri[n], wr4, 0, n, v2_0, start=(i == 0), cols=cols)
         for n in range(N_TILES):
-            acc = psum.tile([P, HALF], F32, name="acc")
-            product(acc, wr4, n, v2_0, start=True)
-            ri.append(acc)
+            one_pass(ri[n], wr4, 1, n, v2_0)
         make_ii(0, v2_0)
-        v2_1 = gather("v2", v2_window, v2_planes, 1)
-        make_ii(1, v2_1)
-        v_0 = gather("v", v_window, v_planes, 0)
+
+        v_0 = (parted_tile("v_parted0"), [picked_tile("v_00"), picked_tile("v_01")])
+        for i, cols in enumerate(pieces):
+            gather_words(v_0[0], v_window, 0, cols, f"words{i}")
+        rr = [psum.tile([P, HALF], F32, name="acc") for n in range(N_TILES)]
+        for a in range(PASSES):
+            gather_scales(v_0[1][a], v_planes, a, 0, whole)
+            for n in range(N_TILES):
+                one_pass(ri[n], wi, a, n, v_0)
+            for n in range(N_TILES):
+                one_pass(rr[n], wr4, a, n, v_0, start=(a == 0))
+
+        for a in range(PASSES):
+            quantise_wrd(a)
+        v2_1 = (parted_tile("v2_parted1"), [picked_tile("words0"), picked_tile("grouped01")])
+        gather_words(v2_1[0], v2_window, 1, whole, "words1")
+        for a in range(PASSES):
+            gather_scales(v2_1[1][a], v2_planes, a, 1, whole)
+
         for n in range(N_TILES):
-            product(ri[n], wi, n, v_0)
-        rr = []
+            one_pass(rr[n], wrd8, 0, n, v_0)
+            one_pass(ri[n], wrd8, 0, n, v2_0)
         for n in range(N_TILES):
-            acc = psum.tile([P, HALF], F32, name="acc")
-            product(acc, wr4, n, v_0, start=True)
-            rr.append(acc)
-        quantise_wrd()
-        v_1 = gather("v", v_window, v_planes, 1)
-        for n in range(N_TILES):
-            product(rr[n], wrd8, n, v_0, stop=True)
-            finish_real(rr[n], 0, n)
-            product(ri[n], wrd8, n, v2_0, stop=True)
+            one_pass(rr[n], wrd8, 1, n, v_0, stop=True)
+            one_pass(ri[n], wrd8, 1, n, v2_0, stop=True)
             finish_imag(ri[n], 0, n)
+            finish_real(rr[n], 0, n)
+
+        v_1 = (parted_tile("v_parted1"), [picked_tile("grouped10"), picked_tile("raw1")])
+        gather_words(v_1[0], v_window, 1, whole, "grouped11")
+        for a in range(PASSES):
+            gather_scales(v_1[1][a], v_planes, a, 1, whole)
+
+        make_ii(1, v2_1)
+        ri = []
+
+        def open_imag(n):
+            acc = psum.tile([P, HALF], F32, name="acc")
+            product(acc, wr4, n, v2_1, start=True)
+            product(acc, wrd8, n, v2_1)
+            ri.append(acc)
+
+        for n in range(N_TILES - 1):
+            open_imag(n)
         for n in range(N_TILES):
             acc = psum.tile([P, HALF], F32, name="acc")
             product(acc, wr4, n, v_1, start=True)
             product(acc, wrd8, n, v_1, stop=True)
             finish_real(acc, 1, n)
-            acc = psum.tile([P, HALF], F32, name="acc")
-            product(acc, wr4, n, v2_1, start=True)
-            product(acc, wrd8, n, v2_1)
-            product(acc, wi, n, v_1, stop=True)
-            finish_imag(acc, 1, n)
+            if n == N_TILES - 1:
+                open_imag(n)
+            product(ri[n], wi, n, v_1, stop=True)
+            finish_imag(ri[n], 1, n)

@@ -31,52 +31,42 @@ def tile_list_cpxtab_dl_crelu_kernel(
     nc = tc.nc
     with ExitStack() as ctx:
         keep = ctx.enter_context(tc.tile_pool(name="keep", bufs=1))
+        reused = ctx.enter_context(tc.tile_pool(name="reused", bufs=1))
         outs = ctx.enter_context(tc.tile_pool(name="outs", bufs=4))
         psum = ctx.enter_context(tc.psum_pool(name="psum", bufs=8))
 
         offsets = keep.tile([P, J // 16], U16, name="offsets")
 
-        def zeroed_plane(name, width, engine):
-            plane = keep.tile([P, PASSES, width], U8, name=name, align_bytes=64)
-            engine.memset(plane[:].bitcast(I32), 0)
+        def zeroed_plane(pool, name, width, offset=None):
+            plane = pool.tile([P, PASSES, width], U8, name=name, align_bytes=64, offset=offset)
+            nc.vector.memset(plane[:].bitcast(I32), 0)
             return plane
 
-        def load_scale_rows(plane, scales, queue, quadrants=range(4)):
-            for q in quadrants:
-                queue.dma_start(
-                    out=plane[32 * q : 32 * q + 4, :, :].bitcast(I32),
-                    in_=scales[:, 4 * q : 4 * q + 4, :].rearrange("a r c -> r a c").bitcast(I32),
-                )
+        def load_scale_rows(plane, scales):
+            by_row = scales.rearrange("a (q r) c -> r q a c", r=4)
+            for r in range(4):
+                nc.sync.dma_start(out=plane[r:P:32, :, :].bitcast(I32), in_=by_row[r].bitcast(I32))
 
-        def load_table_words(name, words):
-            window = keep.tile([P, T], I32, name=name, align_bytes=64)
+        def load_table_words(window, words):
             nc.sync.dma_start(out=window[:], in_=words[0].rearrange("p t b -> p (t b)").bitcast(I32))
-            return window
 
-        wr4_planes = zeroed_plane("wr4_planes", N, nc.gpsimd)
-        v2_planes = zeroed_plane("v2_planes", T, nc.vector)
-        v_planes = zeroed_plane("v_planes", T, nc.vector)
-        wi_planes = zeroed_plane("wi_planes", N, nc.vector)
+        v2_planes = zeroed_plane(keep, "v2_planes", T)
+        wr4_planes = zeroed_plane(keep, "wr4_planes", N)
+        wi_planes = zeroed_plane(keep, "wi_planes", N)
 
         nc.sync.dma_start(offsets[:], offs)
-        v2_window = load_table_words("v2_window", tab2_words)
+        v2_window = keep.tile([P, T], I32, name="v2_window", align_bytes=64)
+        load_table_words(v2_window, tab2_words)
         wr4_codes = keep.tile([P, PASSES, 2 * N], U8, name="wr4_codes", align_bytes=64)
-        nc.sync.dma_start(out=wr4_codes[:].bitcast(I32), in_=wr4_words.rearrange("a p c -> p a c").bitcast(I32))
-        load_scale_rows(wr4_planes, wr4_scales, nc.sync, range(0, 2))
-        load_scale_rows(wr4_planes, wr4_scales, nc.gpsimd, range(2, 4))
-        load_scale_rows(v2_planes, tab2_scales, nc.sync)
-        load_scale_rows(wi_planes, wi_scales, nc.gpsimd, range(2, 4))
-        v_window = load_table_words("v_window", tab_words)
-        load_scale_rows(v_planes, tab_scales, nc.sync)
-        wi_codes = keep.tile([P, PASSES, 4 * N], U8, name="wi_codes", align_bytes=64)
-        nc.sync.dma_start(out=wi_codes[:].bitcast(I32), in_=wi_words.rearrange("a p n i -> p a (n i)").bitcast(I32))
-        load_scale_rows(wi_planes, wi_scales, nc.sync, range(0, 2))
+        nc.sync.dma_start(out=wr4_codes[:].bitcast(I32), in_=wr4_words.bitcast(I32).rearrange("a p c -> p a c"))
+        load_scale_rows(v2_planes, tab2_scales)
+        load_scale_rows(wr4_planes, wr4_scales)
+        load_scale_rows(wi_planes, wi_scales)
 
         def entries(h, cols):
             return offsets[:, (h * HALF + cols.start) // 16 : (h * HALF + cols.stop) // 16]
 
-        def gather_words(parted, window, h, cols, tag):
-            words = keep.tile([P, cols.stop - cols.start], U32, name="words", tag=tag, align_bytes=64)
+        def gather_words(parted, window, h, cols, words):
             nc.vector.tensor_copy(words[:], window[:].bitcast(U32).indirect(entries(h, cols)))
             nc.vector.tensor_copy(
                 parted[:].bitcast(U16)[:, :, cols], words[:].bitcast(U16).rearrange("p (j a) -> p a j", a=PASSES)
@@ -88,30 +78,29 @@ def tile_list_cpxtab_dl_crelu_kernel(
         def parted_tile(name):
             return keep.tile([P, PASSES, 2 * HALF], U8, name=name, align_bytes=64)
 
-        def picked_tile(tag):
-            return keep.tile([P, HALF], U8, name="picked", tag=tag, align_bytes=64)
+        def gather_half(columns, words, window, planes, h):
+            gather_words(columns[0], window, h, slice(0, HALF), words)
+            for a in range(PASSES):
+                gather_scales(columns[1][a], planes, a, h, slice(0, HALF))
+            return columns
+
+        def gather_v(h, tags):
+            words = keep.tile([P, HALF], U32, name=f"v_words{h}", align_bytes=64)
+            picked = [keep.tile([P, HALF], U8, name="v_picked", tag=tag, align_bytes=64) for tag in tags]
+            return gather_half((parted_tile(f"v_parted{h}"), picked), words, v_window, v_planes, h)
 
         wrd_codes = keep.tile([P, PASSES, N], U32, name="wrd_codes", align_bytes=64)
         wrd_planes = keep.tile([P, PASSES, N], U8, name="wrd_planes", align_bytes=64)
 
-        wrd_raw = []
-
-        def load_wrd():
-            for a in range(PASSES):
-                raw = keep.tile([P, 4, N], F32, name=f"wrd_raw{a}", tag=f"raw{a}", align_bytes=64)
-                nc.sync.dma_start(out=raw[:], in_=wrd[512 * a : 512 * (a + 1), :].rearrange("(p i) n -> p i n", i=4))
-                wrd_raw.append(raw)
-
-        def quantise_wrd(a):
-            for u in range(2):
-                cols = slice(u * N // 2, (u + 1) * N // 2)
-                g = keep.tile([P, N // 2, 4], BF16, name="grouped", tag=f"grouped{a}{u}", align_bytes=64)
-                nc.scalar.copy(g[:], wrd_raw[a][:, :, cols].rearrange("p i n -> p n i"))
-                nc.vector.quantize_mx(
-                    out=wrd_codes[:, a, cols].bitcast(FP8X4),
-                    scales=wrd_planes[:, a, cols],
-                    in_=g[:].rearrange("p n i -> p (n i)"),
-                )
+        def quantise_wrd(a, u, copy):
+            cols = slice(u * N // 2, (u + 1) * N // 2)
+            g = keep.tile([P, N // 2, 4], BF16, name="grouped", tag=f"grouped{a}{u}", align_bytes=64)
+            copy(g[:], wrd_raw[:, a, :, cols].rearrange("p i n -> p n i"))
+            nc.vector.quantize_mx(
+                out=wrd_codes[:, a, cols].bitcast(FP8X4),
+                scales=wrd_planes[:, a, cols],
+                in_=g[:].rearrange("p n i -> p (n i)"),
+            )
 
         def wi(a, n):
             return wi_codes[:, a, 4 * M_TILE * n : 4 * M_TILE * (n + 1)].bitcast(FP8X4), wi_planes[:, a, M_TILE * n : M_TILE * (n + 1)]
@@ -137,12 +126,13 @@ def tile_list_cpxtab_dl_crelu_kernel(
 
         ii = {}
 
-        def make_ii(h, v2):
-            for n in range(N_TILES):
-                acc = psum.tile([P, HALF], F32, name="acc")
-                product(acc, wi, n, v2, start=True, stop=True)
-                ii[h, n] = keep.tile([P, HALF], F32, name=f"ii{h}{n}")
-                nc.scalar.copy(ii[h, n][:], acc[:])
+        def make_ii(h, v2, order):
+            accs = [psum.tile([P, HALF], F32, name="acc") for n in range(N_TILES)]
+            for a, n in order:
+                one_pass(accs[n], wi, a, n, v2, start=(a == 0), stop=(a == PASSES - 1))
+                if a == PASSES - 1:
+                    ii[h, n] = keep.tile([P, HALF], F32, name=f"ii{h}{n}")
+                    nc.scalar.copy(ii[h, n][:], accs[n][:])
 
         def finish_real(acc, h, n):
             zr = outs.tile([P, HALF], F32, name="zr")
@@ -162,69 +152,91 @@ def tile_list_cpxtab_dl_crelu_kernel(
         whole = slice(0, HALF)
         pieces = [slice(0, HALF // 2), slice(HALF // 2, HALF)]
 
-        v2_0 = (parted_tile("v2_parted0"), [picked_tile("v2_00"), picked_tile("v2_01")])
+        v2_parted0 = parted_tile("v2_parted0")
+        first_picked = keep.tile([P, HALF], U8, name="first_picked", align_bytes=64)
         for i, cols in enumerate(pieces):
-            gather_words(v2_0[0], v2_window, 0, cols, f"raw{i}")
-            gather_scales(v2_0[1][0], v2_planes, 0, 0, cols)
-        gather_scales(v2_0[1][1], v2_planes, 1, 0, whole)
-        load_wrd()
-        ri = [psum.tile([P, HALF], F32, name="acc") for n in range(N_TILES)]
+            words = reused.tile([P, HALF // 2], U32, name=f"first_words{i}", align_bytes=64, offset=(3584, 20992)[i])
+            gather_words(v2_parted0, v2_window, 0, cols, words)
+            gather_scales(first_picked, v2_planes, 0, 0, cols)
+        staged = reused.tile([P, HALF], U8, name="staged", align_bytes=64, offset=35072)
+        second_picked = keep.tile([P, HALF], U8, name="second_picked", align_bytes=64)
+        gather_scales(staged, v2_planes, 1, 0, whole)
+        nc.vector.tensor_copy(second_picked[:].bitcast(I32), staged[:].bitcast(I32))
+        v2_0 = (v2_parted0, [first_picked, second_picked])
+
+        wi_codes = reused.tile([P, PASSES, 4 * N], U8, name="wi_codes", align_bytes=64, offset=0)
+        nc.sync.dma_start(out=wi_codes[:].bitcast(I32), in_=wi_words.rearrange("a p n i -> p a (n i)").bitcast(I32))
+        wrd_raw = reused.tile([P, PASSES, 4, N], F32, name="wrd_raw", align_bytes=64, offset=5120)
+        for a in range(PASSES):
+            nc.sync.dma_start(
+                out=wrd_raw[:, a, :, :], in_=wrd[512 * a : 512 * (a + 1), :].rearrange("(p i) n -> p i n", i=4)
+            )
+        v_window = reused.tile([P, T], I32, name="v_window", align_bytes=64, offset=21504)
+        load_table_words(v_window, tab_words)
+
+        ri = {}
+        for n in range(N_TILES):
+            ri[0, n] = psum.tile([P, HALF], F32, name="acc")
         for i, cols in enumerate(pieces):
             for n in range(N_TILES):
-                one_pass(ri[n], wr4, 0, n, v2_0, start=(i == 0), cols=cols)
+                one_pass(ri[0, n], wr4, 0, n, v2_0, start=(i == 0), cols=cols)
         for n in range(N_TILES):
-            one_pass(ri[n], wr4, 1, n, v2_0)
-        make_ii(0, v2_0)
+            one_pass(ri[0, n], wr4, 1, n, v2_0)
+        make_ii(0, v2_0, [(a, n) for n in range(N_TILES) for a in range(PASSES)])
 
-        v_0 = (parted_tile("v_parted0"), [picked_tile("v_00"), picked_tile("v_01")])
-        for i, cols in enumerate(pieces):
-            gather_words(v_0[0], v_window, 0, cols, f"words{i}")
-        rr = [psum.tile([P, HALF], F32, name="acc") for n in range(N_TILES)]
+        v2_words1 = reused.tile([P, HALF], U32, name="v2_words1", align_bytes=64, offset=33280)
+        v2_picked1 = reused.tile([P, PASSES, HALF], U8, name="v2_picked1", align_bytes=64, offset=35328)
+        v2_1 = gather_half(
+            (parted_tile("v2_parted1"), [v2_picked1[:, a, :] for a in range(PASSES)]), v2_words1, v2_window, v2_planes, 1
+        )
+        v_planes = zeroed_plane(reused, "v_planes", T, 29696)
+        load_scale_rows(v_planes, tab_scales)
+        v2 = (v2_0, v2_1)
+        make_ii(1, v2_1, [(a, n) for a in range(PASSES) for n in range(N_TILES)])
+        last = N_TILES - 1
+        for n in range(last):
+            ri[1, n] = psum.tile([P, HALF], F32, name="acc")
+            product(ri[1, n], wr4, n, v2_1, start=True)
+
+        quantise_wrd(0, 0, nc.vector.tensor_copy)
+        quantise_wrd(0, 1, nc.vector.tensor_copy)
+        quantise_wrd(1, 0, nc.scalar.copy)
+        quantise_wrd(1, 1, nc.scalar.copy)
         for a in range(PASSES):
-            gather_scales(v_0[1][a], v_planes, a, 0, whole)
             for n in range(N_TILES):
-                one_pass(ri[n], wi, a, n, v_0)
-            for n in range(N_TILES):
-                one_pass(rr[n], wr4, a, n, v_0, start=(a == 0))
+                for h in range(HALVES):
+                    if (h, n) in ri:
+                        one_pass(ri[h, n], wrd8, a, n, v2[h])
 
-        for a in range(PASSES):
-            quantise_wrd(a)
-        v2_1 = (parted_tile("v2_parted1"), [picked_tile("words0"), picked_tile("grouped01")])
-        gather_words(v2_1[0], v2_window, 1, whole, "words1")
-        for a in range(PASSES):
-            gather_scales(v2_1[1][a], v2_planes, a, 1, whole)
-
+        v_0 = gather_v(0, ["v_picked00", "grouped01"])
+        v_1 = gather_v(1, ["grouped10", "grouped11"])
         for n in range(N_TILES):
-            one_pass(rr[n], wrd8, 0, n, v_0)
-            one_pass(ri[n], wrd8, 0, n, v2_0)
+            one_pass(ri[0, n], wi, 0, n, v_0)
+        rr = psum.tile([P, HALF], F32, name="acc")
+        one_pass(rr, wr4, 0, 0, v_0, start=True)
+        one_pass(rr, wrd8, 0, 0, v_0)
         for n in range(N_TILES):
-            one_pass(rr[n], wrd8, 1, n, v_0, stop=True)
-            one_pass(ri[n], wrd8, 1, n, v2_0, stop=True)
-            finish_imag(ri[n], 0, n)
-            finish_real(rr[n], 0, n)
+            one_pass(ri[0, n], wi, 1, n, v_0, stop=True)
+            finish_imag(ri[0, n], 0, n)
+        one_pass(rr, wr4, 1, 0, v_0)
+        one_pass(rr, wrd8, 1, 0, v_0, stop=True)
+        finish_real(rr, 0, 0)
 
-        v_1 = (parted_tile("v_parted1"), [picked_tile("grouped10"), picked_tile("raw1")])
-        gather_words(v_1[0], v_window, 1, whole, "grouped11")
-        for a in range(PASSES):
-            gather_scales(v_1[1][a], v_planes, a, 1, whole)
-
-        make_ii(1, v2_1)
-        ri = []
-
-        def open_imag(n):
+        def real_part(h, n, v):
             acc = psum.tile([P, HALF], F32, name="acc")
-            product(acc, wr4, n, v2_1, start=True)
-            product(acc, wrd8, n, v2_1)
-            ri.append(acc)
+            for a in range(PASSES):
+                one_pass(acc, wr4, a, n, v, start=(a == 0))
+                one_pass(acc, wrd8, a, n, v, stop=(a == PASSES - 1))
+            finish_real(acc, h, n)
 
-        for n in range(N_TILES - 1):
-            open_imag(n)
+        for n in range(1, N_TILES):
+            real_part(0, n, v_0)
+
         for n in range(N_TILES):
-            acc = psum.tile([P, HALF], F32, name="acc")
-            product(acc, wr4, n, v_1, start=True)
-            product(acc, wrd8, n, v_1, stop=True)
-            finish_real(acc, 1, n)
-            if n == N_TILES - 1:
-                open_imag(n)
-            product(ri[n], wi, n, v_1, stop=True)
-            finish_imag(ri[n], 1, n)
+            real_part(1, n, v_1)
+            if n == last:
+                ri[1, n] = psum.tile([P, HALF], F32, name="acc")
+                product(ri[1, n], wr4, n, v2_1, start=True)
+                product(ri[1, n], wrd8, n, v2_1)
+            product(ri[1, n], wi, n, v_1, stop=True)
+            finish_imag(ri[1, n], 1, n)

from contextlib import ExitStack

import concourse.mybir as mybir

K, N, T, J = 1024, 512, 2048, 1024
FLOPS = 6 * 2 * K * N * J

F32 = mybir.dt.float32
BF16 = mybir.dt.bfloat16
I32 = mybir.dt.int32
U32 = mybir.dt.uint32
U16 = mybir.dt.uint16
U8 = mybir.dt.uint8
FP8X4 = mybir.dt.float8_e4m3fn_x4
FP4X4 = mybir.dt.float4_e2m1fn_x4
ACT = mybir.ActivationFunctionType
ALU = mybir.AluOpType

P = 128
PASSES = 2
M_TILE = 128
N_TILES = N // M_TILE
HALF = 512
HALVES = J // HALF


def tile_list_cpxtab_dl_crelu_kernel(
    tc, tab_words, tab_scales, tab2_words, tab2_scales, wr4_words, wr4_scales, wrd, wi_words, wi_scales, offs,
    out_0, out_1,
):
    nc = tc.nc
    with ExitStack() as ctx:
        keep = ctx.enter_context(tc.tile_pool(name="keep", bufs=1))
        reused = ctx.enter_context(tc.tile_pool(name="reused", bufs=1))
        outs = ctx.enter_context(tc.tile_pool(name="outs", bufs=4))
        psum = ctx.enter_context(tc.psum_pool(name="psum", bufs=8))

        offsets = keep.tile([P, J // 16], U16, name="offsets")

        def zeroed_plane(pool, name, width, offset=None):
            plane = pool.tile([P, PASSES, width], U8, name=name, align_bytes=64, offset=offset)
            nc.vector.memset(plane[:].bitcast(I32), 0)
            return plane

        def load_scale_rows(plane, scales):
            by_row = scales.rearrange("a (q r) c -> r q a c", r=4)
            for r in range(4):
                nc.sync.dma_start(out=plane[r:P:32, :, :].bitcast(I32), in_=by_row[r].bitcast(I32))

        def load_table_words(window, words):
            nc.sync.dma_start(out=window[:], in_=words[0].rearrange("p t b -> p (t b)").bitcast(I32))

        v2_planes = zeroed_plane(keep, "v2_planes", T)
        wr4_planes = zeroed_plane(keep, "wr4_planes", N)
        wi_planes = zeroed_plane(keep, "wi_planes", N)

        nc.sync.dma_start(offsets[:], offs)
        v2_window = keep.tile([P, T], I32, name="v2_window", align_bytes=64)
        load_table_words(v2_window, tab2_words)
        wr4_codes = keep.tile([P, PASSES, 2 * N], U8, name="wr4_codes", align_bytes=64)
        nc.sync.dma_start(out=wr4_codes[:].bitcast(I32), in_=wr4_words.bitcast(I32).rearrange("a p c -> p a c"))
        load_scale_rows(v2_planes, tab2_scales)
        load_scale_rows(wr4_planes, wr4_scales)
        load_scale_rows(wi_planes, wi_scales)

        def entries(h, cols):
            return offsets[:, (h * HALF + cols.start) // 16 : (h * HALF + cols.stop) // 16]

        def gather_words(parted, window, h, cols, words):
            nc.vector.tensor_copy(words[:], window[:].bitcast(U32).indirect(entries(h, cols)))
            nc.vector.tensor_copy(
                parted[:].bitcast(U16)[:, :, cols], words[:].bitcast(U16).rearrange("p (j a) -> p a j", a=PASSES)
            )

        def gather_scales(picked, planes, a, h, cols):
            nc.vector.tensor_copy(picked[:, cols], planes[:, a, :].indirect(entries(h, cols)))

        def parted_tile(name):
            return keep.tile([P, PASSES, 2 * HALF], U8, name=name, align_bytes=64)

        def gather_half(columns, words, window, planes, h):
            gather_words(columns[0], window, h, slice(0, HALF), words)
            for a in range(PASSES):
                gather_scales(columns[1][a], planes, a, h, slice(0, HALF))
            return columns

        def gather_v(h, tags):
            words = keep.tile([P, HALF], U32, name=f"v_words{h}", align_bytes=64)
            picked = [keep.tile([P, HALF], U8, name="v_picked", tag=tag, align_bytes=64) for tag in tags]
            return gather_half((parted_tile(f"v_parted{h}"), picked), words, v_window, v_planes, h)

        wrd_codes = keep.tile([P, PASSES, N], U32, name="wrd_codes", align_bytes=64)
        wrd_planes = keep.tile([P, PASSES, N], U8, name="wrd_planes", align_bytes=64)

        def quantise_wrd(a, u, copy):
            cols = slice(u * N // 2, (u + 1) * N // 2)
            g = keep.tile([P, N // 2, 4], BF16, name="grouped", tag=f"grouped{a}{u}", align_bytes=64)
            copy(g[:], wrd_raw[:, a, :, cols].rearrange("p i n -> p n i"))
            nc.vector.quantize_mx(
                out=wrd_codes[:, a, cols].bitcast(FP8X4),
                scales=wrd_planes[:, a, cols],
                in_=g[:].rearrange("p n i -> p (n i)"),
            )

        def wi(a, n):
            return wi_codes[:, a, 4 * M_TILE * n : 4 * M_TILE * (n + 1)].bitcast(FP8X4), wi_planes[:, a, M_TILE * n : M_TILE * (n + 1)]

        def wr4(a, n):
            return wr4_codes[:, a, 2 * M_TILE * n : 2 * M_TILE * (n + 1)].bitcast(FP4X4), wr4_planes[:, a, M_TILE * n : M_TILE * (n + 1)]

        def wrd8(a, n):
            return wrd_codes[:, a, M_TILE * n : M_TILE * (n + 1)].bitcast(FP8X4), wrd_planes[:, a, M_TILE * n : M_TILE * (n + 1)]

        def one_pass(acc, weight, a, n, columns, start=False, stop=False, cols=slice(0, HALF)):
            codes, scales = weight(a, n)
            parted, picked = columns
            nc.tensor.matmul_mx(
                out=acc[:, cols], lhsT=codes, lhsT_scale=scales,
                rhs=parted[:, a, 2 * cols.start : 2 * cols.stop].bitcast(FP4X4), rhs_scale=picked[a][:, cols],
                start=start, stop=stop,
            )

        def product(acc, weight, n, columns, start=False, stop=False):
            for a in range(PASSES):
                one_pass(acc, weight, a, n, columns, start and a == 0, stop and a == PASSES - 1)

        ii = {}

        def make_ii(h, v2, order):
            accs = [psum.tile([P, HALF], F32, name="acc") for n in range(N_TILES)]
            for a, n in order:
                one_pass(accs[n], wi, a, n, v2, start=(a == 0), stop=(a == PASSES - 1))
                if a == PASSES - 1:
                    ii[h, n] = keep.tile([P, HALF], F32, name=f"ii{h}{n}")
                    nc.scalar.copy(ii[h, n][:], accs[n][:])

        def finish_real(acc, h, n):
            zr = outs.tile([P, HALF], F32, name="zr")
            nc.vector.tensor_tensor(zr[:], acc[:], ii[h, n][:], ALU.subtract)
            res = outs.tile([P, HALF], F32, name="res0")
            if h == 0:
                nc.scalar.activation(res[:], zr[:], ACT.Relu)
            else:
                nc.vector.tensor_scalar_max(res[:], zr[:], 0.0)
            nc.sync.dma_start(out=out_0[M_TILE * n : M_TILE * (n + 1), HALF * h : HALF * (h + 1)], in_=res[:])

        def finish_imag(acc, h, n):
            res = outs.tile([P, HALF], F32, name="res1")
            nc.scalar.activation(res[:], acc[:], ACT.Relu)
            nc.sync.dma_start(out=out_1[M_TILE * n : M_TILE * (n + 1), HALF * h : HALF * (h + 1)], in_=res[:])

        whole = slice(0, HALF)
        pieces = [slice(0, HALF // 2), slice(HALF // 2, HALF)]

        v2_parted0 = parted_tile("v2_parted0")
        first_picked = keep.tile([P, HALF], U8, name="first_picked", align_bytes=64)
        for i, cols in enumerate(pieces):
            words = reused.tile([P, HALF // 2], U32, name=f"first_words{i}", align_bytes=64, offset=(3584, 20992)[i])
            gather_words(v2_parted0, v2_window, 0, cols, words)
            gather_scales(first_picked, v2_planes, 0, 0, cols)
        staged = reused.tile([P, HALF], U8, name="staged", align_bytes=64, offset=35072)
        second_picked = keep.tile([P, HALF], U8, name="second_picked", align_bytes=64)
        gather_scales(staged, v2_planes, 1, 0, whole)
        nc.vector.tensor_copy(second_picked[:].bitcast(I32), staged[:].bitcast(I32))
        v2_0 = (v2_parted0, [first_picked, second_picked])

        wi_codes = reused.tile([P, PASSES, 4 * N], U8, name="wi_codes", align_bytes=64, offset=0)
        nc.sync.dma_start(out=wi_codes[:].bitcast(I32), in_=wi_words.rearrange("a p n i -> p a (n i)").bitcast(I32))
        wrd_raw = reused.tile([P, PASSES, 4, N], F32, name="wrd_raw", align_bytes=64, offset=5120)
        for a in range(PASSES):
            nc.sync.dma_start(
                out=wrd_raw[:, a, :, :], in_=wrd[512 * a : 512 * (a + 1), :].rearrange("(p i) n -> p i n", i=4)
            )
        v_window = reused.tile([P, T], I32, name="v_window", align_bytes=64, offset=21504)
        load_table_words(v_window, tab_words)

        ri = {}
        for n in range(N_TILES):
            ri[0, n] = psum.tile([P, HALF], F32, name="acc")
        for i, cols in enumerate(pieces):
            for n in range(N_TILES):
                one_pass(ri[0, n], wr4, 0, n, v2_0, start=(i == 0), cols=cols)
        for n in range(N_TILES):
            one_pass(ri[0, n], wr4, 1, n, v2_0)
        make_ii(0, v2_0, [(a, n) for n in range(N_TILES) for a in range(PASSES)])

        v2_words1 = reused.tile([P, HALF], U32, name="v2_words1", align_bytes=64, offset=33280)
        v2_picked1 = reused.tile([P, PASSES, HALF], U8, name="v2_picked1", align_bytes=64, offset=35328)
        v2_1 = gather_half(
            (parted_tile("v2_parted1"), [v2_picked1[:, a, :] for a in range(PASSES)]), v2_words1, v2_window, v2_planes, 1
        )
        v_planes = zeroed_plane(reused, "v_planes", T, 29696)
        load_scale_rows(v_planes, tab_scales)
        v2 = (v2_0, v2_1)
        make_ii(1, v2_1, [(a, n) for a in range(PASSES) for n in range(N_TILES)])
        last = N_TILES - 1
        for n in range(last):
            ri[1, n] = psum.tile([P, HALF], F32, name="acc")
            product(ri[1, n], wr4, n, v2_1, start=True)

        quantise_wrd(0, 0, nc.vector.tensor_copy)
        quantise_wrd(0, 1, nc.vector.tensor_copy)
        quantise_wrd(1, 0, nc.scalar.copy)
        quantise_wrd(1, 1, nc.scalar.copy)
        for a in range(PASSES):
            for n in range(N_TILES):
                for h in range(HALVES):
                    if (h, n) in ri:
                        one_pass(ri[h, n], wrd8, a, n, v2[h])

        v_0 = gather_v(0, ["v_picked00", "grouped01"])
        v_1 = gather_v(1, ["grouped10", "grouped11"])
        for n in range(N_TILES):
            one_pass(ri[0, n], wi, 0, n, v_0)
        rr = psum.tile([P, HALF], F32, name="acc")
        one_pass(rr, wr4, 0, 0, v_0, start=True)
        one_pass(rr, wrd8, 0, 0, v_0)
        for n in range(N_TILES):
            one_pass(ri[0, n], wi, 1, n, v_0, stop=True)
            finish_imag(ri[0, n], 0, n)
        one_pass(rr, wr4, 1, 0, v_0)
        one_pass(rr, wrd8, 1, 0, v_0, stop=True)
        finish_real(rr, 0, 0)

        def real_part(h, n, v):
            acc = psum.tile([P, HALF], F32, name="acc")
            for a in range(PASSES):
                one_pass(acc, wr4, a, n, v, start=(a == 0))
                one_pass(acc, wrd8, a, n, v, stop=(a == PASSES - 1))
            finish_real(acc, h, n)

        for n in range(1, N_TILES):
            real_part(0, n, v_0)

        for n in range(N_TILES):
            real_part(1, n, v_1)
            if n == last:
                ri[1, n] = psum.tile([P, HALF], F32, name="acc")
                product(ri[1, n], wr4, n, v2_1, start=True)
                product(ri[1, n], wrd8, n, v2_1)
            product(ri[1, n], wi, n, v_1, stop=True)
            finish_imag(ri[1, n], 1, n)
